import numpy as np, ml_dtypes
CORES = [23,119,17,113]
N = 4
import mx_ref
NC, G, D = 256, 4, 32
C = np.float32(0.029)
BF = ml_dtypes.bfloat16
def cut(t, i, w=512):
    return t[:, w * i:w * i + w]
def tile(rs):
    return np.stack(rs, axis=2).reshape(128, -1).astype(BF)
def act(Z):
    return [np.maximum(z, 0) * C for z in Z]
def taps(w, i, e):
    return mx_ref.matmul(mx_ref.quantize(cut(w, 2 * i)), mx_ref.quantize(e[:, :4 * NC])) + mx_ref.matmul(mx_ref.quantize(cut(w, 2 * i + 1)), mx_ref.quantize(e[:, 4 * D:4 * D + 4 * NC]))
def setup_inputs(rng):
    def f(*shape):
        return mx_ref.flush((rng.standard_normal(shape, dtype=np.float32) * np.exp2(rng.integers(-2, 3, shape[:-1] + (1,)))).astype(BF))
    return {"x": f(N, 128, 4 * NC), "wa": np.broadcast_to(f(1, 128, 2 * G * 512), (N, 128, 2 * G * 512)).copy(), "wb": f(N, 128, 2 * 512)}
def setup_inputs_blocks(rng):
    d = setup_inputs(rng)
    for k in ("x", "wb"): d[k] = mx_ref.spread(d[k], rng, 2)
    return d
def setup_inputs_wide(rng):
    d = setup_inputs(rng)
    for k in ("wb",): d[k] = mx_ref.flush((d[k].astype(np.float32) * np.exp2(rng.integers(-6, 7, (N, 1, 1))).astype(np.float32)).astype(BF))
    return d
def setup_inputs_zeros(rng):
    d = setup_inputs(rng); v = d["x"].reshape(N, 128, -1, 4).copy()
    v[np.broadcast_to((rng.random((N, 1, v.shape[2], 1)) < 0.33), v.shape)] = 0
    d["x"] = v.reshape(d["x"].shape)
    return d
def reference(x, wa, wb):
    edge = lambda t, r: np.concatenate([t[(r - 1) % N][:, 4 * (NC - D):], t[r]], axis=1)
    u = [tile(act([taps(wa[r], i, edge(x, r)) for i in range(G)])) for r in range(N)]
    y = np.zeros((N, 128, NC), np.float32)
    for r in range(N):
        y[r] = taps(wb[r], 0, edge(u, r))
    return {"y": y}

import numpy as np
from concourse.mybir import dt, AluOpType, ActivationFunctionType

SCRATCH = {
    "xt": ("sbuf", [128, 512], "bfloat16"),
    "xr": ("sbuf", [128, 512], "bfloat16"),
    "wat": ("sbuf", [128, 4096], "bfloat16"),
    "wbt": ("sbuf", [128, 1024], "bfloat16"),
    "ut": ("sbuf", [128, 1152], "bfloat16"),
    "qx": ("sbuf", [128, 320], "float8_e4m3fn_x4"),
    "sx": ("sbuf", [128, 320], "uint8"),
    "qw": ("sbuf", [128, 1024], "float8_e4m3fn_x4"),
    "sw": ("sbuf", [128, 1024], "uint8"),
    "qb": ("sbuf", [128, 256], "float8_e4m3fn_x4"),
    "sb": ("sbuf", [128, 256], "uint8"),
    "qu": ("sbuf", [128, 288], "float8_e4m3fn_x4"),
    "su": ("sbuf", [128, 288], "uint8"),
    "yo": ("sbuf", [128, 256], "float32"),
    "ps": ("psum", [128, 4096], "float32"),
}
PIECES = [(0, 2), (2, 4), (4, 6), (6, 8)]
SEMAPHORES = (["ld_xt", "ld_xr", "ld_wb", "first", "halo", "sent", "q_xt", "q_xr", "q_wb", "q_ua", "q_ub",
               "my_a", "my_b", "c_a", "c_b", "st_a", "st_b"]
              + ["ld_w%d" % k for k in range(len(PIECES))] + ["q_w%d" % k for k in range(8)]
              + ["m%s%d" % (h, b) for h in "AB" for b in range(4)] + ["a%s%d" % (h, b) for h in "AB" for b in range(4)])

CACT = float(np.float32(0.029))
H = 64
TAP = 32
PART = {"A": (0, 128, 4), "B": (128, 288, 0)}


def rank_program(g, core, T, topo):
    rank = T.rank_of(core)
    if rank is None:
        return
    S = T.sem
    nxt = T.cores[(rank + 1) % len(T.cores)]
    relu = ActivationFunctionType.Relu

    def bank(k, n):
        return T.ps[:, 512 * k:512 * k + n]

    def load_w(q, k):
        a, b = PIECES[k]
        q.dma_start(T.wat[:, 512 * a:512 * b], T.wa[:, 512 * a:512 * b]).then_inc(S["ld_w%d" % k], 16)

    g.sync.dma_start(T.xt[:], T.x[:, 512:1024]).then_inc(S.ld_xt, 16)
    g.sync.sem_inc(S.first, 1)
    g.scalar.wait_ge(S.first, 1)
    g.sync.dma_start(T.xr[:], T.x[:, 0:512]).then_inc(S.ld_xr, 16)
    load_w(g.scalar, 0)
    load_w(g.sync, 1)
    load_w(g.scalar, 2)
    load_w(g.sync, 3)
    g.scalar.dma_start(T.wbt[:], T.wb[:]).then_inc(S.ld_wb, 16)

    m = topo.mask(core, nxt)
    rid, pid, _se = topo.addr(nxt)
    n_eng = bin(m).count("1")
    own = slice(256, 256 + H)
    g.wait_ge(S.q_xt, 1)
    g.remote_dma(T.qx[:, 0:H].bitcast(dt.uint8), T.qx[:, own].bitcast(dt.uint8), S.halo, S.sent, pid, rid, m)
    g.remote_dma(T.sx[:, 0:H], T.sx[:, own], S.halo, S.sent, pid, rid, m)
    g.wait_ge(S.sent, 2 * n_eng)

    def act_s(h, b):
        lo, hi, k = PART[h]
        g.scalar.wait_ge(S["m%s%d" % (h, b)], 1)
        g.scalar.activation(T.ut[:, 4 * lo + b:4 * hi:4], bank(k + b, hi - lo), relu,
                            scale=CACT).then_inc(S["a%s%d" % (h, b)], 1)

    def act_v(h, b):
        lo, hi, k = PART[h]
        g.vector.wait_ge(S["m%s%d" % (h, b)], 1)
        g.vector.tensor_scalar(T.ut[:, 4 * lo + b:4 * hi:4], bank(k + b, hi - lo), 0.0, CACT,
                               AluOpType.max, AluOpType.mult).then_inc(S["a%s%d" % (h, b)], 1)

    def quant_u(h, sem):
        lo, hi, k = PART[h]
        for b in range(4):
            g.vector.wait_ge(S["a%s%d" % (h, b)], 1)
        g.vector.quantize_mx(T.qu[:, lo:hi], T.su[:, lo:hi], T.ut[:, 4 * lo:4 * hi]).then_inc(sem, 1)

    v = g.vector
    v.wait_ge(S.ld_xt, 16)
    v.quantize_mx(T.qx[:, 192:320], T.sx[:, 192:320], T.xt[:]).then_inc(S.q_xt, 1)
    v.wait_ge(S.ld_xr, 16)
    v.quantize_mx(T.qx[:, 64:192], T.sx[:, 64:192], T.xr[:]).then_inc(S.q_xr, 1)
    for k, (a, b) in enumerate(PIECES):
        v.wait_ge(S["ld_w%d" % k], 16)
        for t in range(a, b):
            v.quantize_mx(T.qw[:, 128 * t:128 * t + 128], T.sw[:, 128 * t:128 * t + 128],
                          T.wat[:, 512 * t:512 * t + 512]).then_inc(S["q_w%d" % t], 1)
    act_v("B", 3)
    quant_u("B", S.q_ub)
    v.wait_ge(S.ld_wb, 16)
    v.quantize_mx(T.qb[:], T.sb[:], T.wbt[:]).then_inc(S.q_wb, 1)
    act_v("A", 1)
    act_v("A", 3)
    quant_u("A", S.q_ua)
    v.wait_ge(S.my_a, 1)
    v.tensor_copy(T.yo[:, 0:128], bank(1, 128)).then_inc(S.c_a, 1)

    for b in range(3):
        act_s("B", b)
    act_s("A", 0)
    act_s("A", 2)
    g.scalar.wait_ge(S.my_b, 1)
    g.scalar.activation(T.yo[:, 128:256], bank(0, 128), ActivationFunctionType.Copy).then_inc(S.c_b, 1)

    te = g.tensor

    def layer1(h):
        lo, hi, k = PART[h]
        for t in range(8):
            b, tap = divmod(t, 2)
            if h == "B":
                te.wait_ge(S["q_w%d" % t], 1)
            mm = te.matmul_mx(bank(k + b, hi - lo), T.qw[:, 128 * t:128 * t + 128], T.sw[:, 128 * t:128 * t + 128],
                              T.qx[:, lo + TAP * tap:hi + TAP * tap], T.sx[:, lo + TAP * tap:hi + TAP * tap],
                              tap == 0, tap == 1)
            if tap == 1:
                mm.then_inc(S["m%s%d" % (h, b)], 1)

    def layer2(lo, k, sem):
        for tap in range(2):
            mm = te.matmul_mx(bank(k, 128), T.qb[:, 128 * tap:128 * tap + 128], T.sb[:, 128 * tap:128 * tap + 128],
                              T.qu[:, lo + TAP * tap:lo + TAP * tap + 128], T.su[:, lo + TAP * tap:lo + TAP * tap + 128],
                              tap == 0, tap == 1)
        mm.then_inc(sem, 1)

    te.wait_ge(S.q_xt, 1)
    te.wait_ge(S.q_xr, 1)
    layer1("B")
    te.wait_ge(S.halo, 2 * n_eng)
    layer1("A")
    te.wait_ge(S.q_ub, 1)
    te.wait_ge(S.q_wb, 1)
    layer2(128, 0, S.my_b)
    te.wait_ge(S.q_ua, 1)
    layer2(0, 1, S.my_a)

    g.scalar.wait_ge(S.c_b, 1)
    g.scalar.dma_start(T.y[:, 128:256], T.yo[:, 128:256]).then_inc(S.st_b, 16)
    g.sync.wait_ge(S.c_a, 1)
    g.sync.dma_start(T.y[:, 0:128], T.yo[:, 0:128]).then_inc(S.st_a, 16)
    g.scalar.wait_ge(S.st_b, 16)
    g.sync.wait_ge(S.st_a, 16)
